import numpy as np
import ml_dtypes


def mxq(x, axis, fmt="e4m3"):
    dtype, down = {"e4m3": (ml_dtypes.float8_e4m3fn, 7), "e5m2": (ml_dtypes.float8_e5m2, 14)}[fmt]
    v = np.moveaxis(np.asarray(x, np.float32).astype(ml_dtypes.bfloat16).astype(np.float64), axis, -1)
    blocks = v.reshape(v.shape[:-1] + (-1, 32))
    amax = np.abs(blocks).max(-1, keepdims=True)
    byte = np.maximum(np.where(amax > 0, np.frexp(amax)[1] - 1 + 127, 0) - down, 1)
    scale = np.exp2(byte - 127.0)
    codes = (blocks / scale).astype(np.float32).astype(dtype).astype(np.float64)
    return np.moveaxis((codes * scale).reshape(v.shape), -1, axis)


WIDE = False


def mx_kscale(k):
    if not WIDE:
        return np.ones(k)
    levels = np.array([10, -10, 5, -5, 0])
    if k % 512:
        return np.exp2(np.random.permutation(np.resize(levels, k // 32))).repeat(32)
    a = np.empty((k // 512, 16))
    for p in range(k // 512):
        a[p, :8] = np.random.permutation(np.resize(levels, 8))
        for g in range(8):
            far = levels[np.abs(levels - a[p, g]) >= 10]
            a[p, g + 8] = far[np.random.randint(len(far))]
    return np.exp2(a.ravel()).repeat(32)


def f64(x):
    return np.asarray(x).astype(np.float64)


def striped(idx):
    return np.tile(idx.reshape(-1, 16).T, (8, 1)).astype(np.uint16)


def unstriped(offs):
    return offs[:16].T.reshape(-1).astype(np.int64)


E2M1 = np.array([0.0, 0.5, 1.0, 1.5, 2.0, 3.0, 4.0, 6.0, -0.0, -0.5, -1.0, -1.5, -2.0, -3.0, -4.0, -6.0])


def pack_weight(w, fmt):
    k, n = w.shape
    w = f64(np.asarray(w, np.float32).astype(ml_dtypes.bfloat16)).reshape(k // 32, 32, n)
    amax = np.abs(w).max(1)
    if fmt == "e4m3":
        byte = np.frexp(amax)[1] - 1 + 127 - 7
    else:
        mant, ex = np.frexp(amax / 6.0)
        byte = np.where(mant > 0.5, ex, ex - 1) + 127
    byte = np.clip(np.where(amax > 0, byte, 1), 1, 254)
    scaled = (w * np.exp2(127.0 - byte)[:, None, :]).reshape(k, n).astype(np.float32)
    by_word = np.ascontiguousarray(scaled.reshape(k // 512, 128, 4, n).transpose(0, 1, 3, 2))
    if fmt == "e4m3":
        words = by_word.astype(ml_dtypes.float8_e4m3fn).view(np.uint8)
    else:
        c = by_word.astype(ml_dtypes.float4_e2m1fn).view(np.uint8) & 0xF
        words = (c[..., 0::2] | (c[..., 1::2] << 4)).reshape(k // 512, 128, 2 * n)
    return np.ascontiguousarray(words), np.ascontiguousarray(byte.astype(np.uint8).reshape(k // 512, 16, n))


def unpack_weight(words, scales, fmt):
    g, _, n = scales.shape
    words = np.ascontiguousarray(words).reshape(g, 128, n, -1)
    if fmt == "e4m3":
        vals = words.view(ml_dtypes.float8_e4m3fn).astype(np.float64)
    else:
        nib = np.empty((g, 128, n, 4), np.uint8)
        nib[..., 0::2] = words & 0xF
        nib[..., 1::2] = words >> 4
        vals = E2M1[nib]
    vals = vals * np.repeat(np.exp2(scales.astype(np.float64) - 127.0), 8, axis=1)[..., None]
    return vals.transpose(0, 1, 3, 2).reshape(g * 512, n)


def sigmoid(v):
    return 1.0 / (1.0 + np.exp(-np.maximum(v, -700.0)))


K, T, E, C, H, N = 512, 1280, 6, 128, 512, 128


def by_expert(wq, xq):
    return np.concatenate([wq[e].T @ xq[:, e * C:(e + 1) * C] for e in range(E)], axis=1)


def setup_inputs():
    n = np.random.standard_normal
    s = mx_kscale(K)[:, None]
    u = mx_kscale(H)
    w1 = [pack_weight(m, "e2m1") for m in n((E + 1, K, H)) / np.sqrt(K) / s[None]]
    w3 = [pack_weight(m, "e2m1") for m in n((E + 1, K, H)) / np.sqrt(K) / s[None] * u[None, None, :]]
    w2 = [pack_weight(m, "e2m1") for m in n((E + 1, H, N)) / np.sqrt(H) / u[None, :, None]]
    x = pack_weight(n((K, T)) * s, "e4m3")
    return {
        "x_words": x[0],
        "x_scales": x[1],
        "w1_words": np.stack([m[0] for m in w1]),
        "w1_scales": np.stack([m[1] for m in w1]),
        "w3_words": np.stack([m[0] for m in w3]),
        "w3_scales": np.stack([m[1] for m in w3]),
        "w2_words": np.stack([m[0] for m in w2]),
        "w2_scales": np.stack([m[1] for m in w2]),
        "gate": np.tile(np.random.uniform(0.2, 1.0, E * C), (N, 1)).astype(np.float32),
        "offs": striped(np.random.permutation(T)[:E * C]),
    }


def reference(x_words, x_scales, w1_words, w1_scales, w3_words, w3_scales, w2_words, w2_scales, gate, offs):
    idx = unstriped(offs)
    w1 = np.stack([unpack_weight(w1_words[e], w1_scales[e], "e2m1") for e in range(E + 1)])
    w3 = np.stack([unpack_weight(w3_words[e], w3_scales[e], "e2m1") for e in range(E + 1)])
    w2 = np.stack([unpack_weight(w2_words[e], w2_scales[e], "e2m1") for e in range(E + 1)])
    w1q, w3q, w2q = w1, w3, w2
    xs = unpack_weight(x_words, x_scales, "e4m3")
    hs = sigmoid(w1q[E].T @ xs) * (w3q[E].T @ xs)
    ys = w2q[E].T @ mxq(hs, 0, "e4m3")
    xq = unpack_weight(x_words, x_scales, "e4m3")[:, idx]
    h = sigmoid(by_expert(w1q, xq))
    h = h * by_expert(w3q, xq)
    y = by_expert(w2q, mxq(h, 0, "e4m3"))
    out = ys
    out[:, idx] += f64(gate) * y
    return out

@@ -1,0 +1,244 @@
+from contextlib import ExitStack
+
+import concourse.mybir as mybir
+from concourse.masks import make_identity
+
+K, T, E, C, H, N = 512, 1280, 6, 128, 512, 128
+SLOTS = E * C
+FLOPS = 2 * (SLOTS + T) * (2 * K * H + H * N)
+
+F32 = mybir.dt.float32
+BF16 = mybir.dt.bfloat16
+I32 = mybir.dt.int32
+U32 = mybir.dt.uint32
+U16 = mybir.dt.uint16
+U8 = mybir.dt.uint8
+FP8X4 = mybir.dt.float8_e4m3fn_x4
+FP4X4 = mybir.dt.float4_e2m1fn_x4
+MULT = mybir.AluOpType.mult
+ADD = mybir.AluOpType.add
+SIGMOID = mybir.ActivationFunctionType.Sigmoid
+
+P = 128
+BLOCK = 128
+BANK = 512
+
+
+def tile_moe_shr_glu_sigmoid_kernel(
+    tc, x_words, x_scales, w1_words, w1_scales, w3_words, w3_scales, w2_words, w2_scales, gate, offs, out
+):
+    nc = tc.nc
+    with ExitStack() as ctx:
+        keep = ctx.enter_context(tc.tile_pool(name="keep", bufs=1))
+        ring = ctx.enter_context(tc.tile_pool(name="ring", bufs=6))
+        psum = ctx.enter_context(tc.psum_pool(name="psum", bufs=1))
+
+        offsets = keep.tile([P, SLOTS // 16], U16, name="offsets")
+        xw = keep.tile([P, T], I32, name="xw", align_bytes=64)
+        xs = keep.tile([P, T], U8, name="xs", align_bytes=64)
+
+        def plane(name, width):
+            t = keep.tile([P, width], U8, name=name, align_bytes=64)
+            nc.vector.memset(t[:].bitcast(I32), 0)
+            return t
+
+        def load_scales(t, src, e0, e1):
+            for r in range(4):
+                nc.sync.dma_start(
+                    out=t[:].bitcast(I32)[r:P:32, :].rearrange("q (e n) -> q e n", e=e1 - e0),
+                    in_=src[e0:e1, 0, r:16:4, :].rearrange("e q n -> q e n").bitcast(I32),
+                )
+
+        def load_words(name, src, e0, e1):
+            width = src.shape[3]
+            t = keep.tile([P, (e1 - e0) * width], U8, name=name, align_bytes=64)
+            nc.sync.dma_start(
+                out=t[:].bitcast(I32).rearrange("p (e n) -> p e n", e=e1 - e0),
+                in_=src[e0:e1, 0, :, :].rearrange("e p n -> p e n").bitcast(I32),
+            )
+            return t
+
+        nc.vector.memset(xs[:].bitcast(I32), 0)
+        scale_groups = [(0, 3), (3, 7)]
+        word_groups = [(0, 2), (2, 4), (4, 7)]
+        s1 = [plane("s1_%d" % g, (e1 - e0) * H) for g, (e0, e1) in enumerate(scale_groups[:1])]
+        s3 = [plane("s3_%d" % g, (e1 - e0) * H) for g, (e0, e1) in enumerate(scale_groups[:1])]
+        s1 = s1 + [plane("s1_%d" % (g + 1), (e1 - e0) * H) for g, (e0, e1) in enumerate(scale_groups[1:])]
+        s3 = s3 + [plane("s3_%d" % (g + 1), (e1 - e0) * H) for g, (e0, e1) in enumerate(scale_groups[1:])]
+        s2 = plane("s2", (E + 1) * N)
+        routed = keep.tile([P, T], F32, name="routed")
+        nc.vector.memset(routed[:], 0.0)
+        ident = keep.tile([P, P], F32, name="ident")
+        make_identity(nc, ident[:])
+        warm = keep.tile([P, 8], F32, name="warm")
+        nc.scalar.activation(warm[:], ident[:, 0:8], SIGMOID)
+
+        nc.sync.dma_start(out=xw[:], in_=x_words[0].rearrange("p t r -> p (t r)").bitcast(I32))
+        nc.sync.dma_start(offsets[:], offs)
+        for r in range(4):
+            nc.sync.dma_start(out=xs[:].bitcast(I32)[r:P:32, :], in_=x_scales[0, r:16:4, :].bitcast(I32))
+        w1 = [load_words("w1_0", w1_words, *word_groups[0])]
+        w3 = [load_words("w3_0", w3_words, *word_groups[0])]
+        load_scales(s1[0], w1_scales, *scale_groups[0])
+        load_scales(s3[0], w3_scales, *scale_groups[0])
+        w1.append(load_words("w1_1", w1_words, *word_groups[1]))
+        w3.append(load_words("w3_1", w3_words, *word_groups[1]))
+        for g in range(1, len(scale_groups)):
+            load_scales(s1[g], w1_scales, *scale_groups[g])
+            load_scales(s3[g], w3_scales, *scale_groups[g])
+        w2 = load_words("w2", w2_words, 0, E + 1)
+        load_scales(s2, w2_scales, 0, E + 1)
+        for g in range(2, len(word_groups)):
+            w1.append(load_words("w1_%d" % g, w1_words, *word_groups[g]))
+            w3.append(load_words("w3_%d" % g, w3_words, *word_groups[g]))
+        gates = keep.tile([P, SLOTS], F32, name="gates")
+        nc.sync.dma_start(out=gates[:], in_=gate)
+
+        def pick(tiles, groups, e, width):
+            for t, (e0, e1) in zip(tiles, groups):
+                if e0 <= e < e1:
+                    return t[:, (e - e0) * width : (e - e0 + 1) * width]
+
+        cuts = [(0, 256), (256, 768)]
+        gw, gs = [], []
+        for g, (a, b) in enumerate(cuts):
+            tw = keep.tile([P, b - a], U32, name="gw%d" % g, align_bytes=64)
+            ts = keep.tile([P, b - a], U8, name="gs%d" % g, align_bytes=64)
+            nc.vector.tensor_copy(tw[:], xw[:].bitcast(U32).indirect(offsets[:, a // 16 : b // 16]))
+            nc.vector.tensor_copy(ts[:], xs[:].indirect(offsets[:, a // 16 : b // 16]))
+            gw.append(tw)
+            gs.append(ts)
+
+        ring_s = [psum.tile([P, BANK], F32, name="s%d" % i) for i in range(5)]
+        bank_b = [psum.tile([P, BANK], F32, name="b%d" % i) for i in range(3)]
+        taken = []
+
+        def next_s():
+            taken.append(0)
+            return ring_s[len(taken) % len(ring_s)]
+
+        begun = []
+
+        def next_b():
+            begun.append(0)
+            return bank_b[len(begun) % len(bank_b)]
+
+        hw = keep.tile([P, SLOTS + T], U32, name="hw", align_bytes=64)
+        hs = keep.tile([P, SLOTS + T], U8, name="hs", align_bytes=64)
+        y = keep.tile([P, SLOTS], F32, name="y")
+
+        def operand(j):
+            if j < E:
+                for tw, ts, (a, b) in zip(gw, gs, cuts):
+                    if a <= j * C < b:
+                        cols = slice(j * C - a, (j + 1) * C - a)
+                        return tw[:, cols], ts[:, cols], j
+            cols = slice((j - E) * BLOCK, (j - E + 1) * BLOCK)
+            return xw[:, cols], xs[:, cols], E
+
+        hidden = {}
+
+        def first(j):
+            words, scales, e = operand(j)
+            a = next_s()
+            b = next_b()
+            for acc, wt, st in ((a, w1, s1), (b, w3, s3)):
+                nc.tensor.matmul_mx(
+                    out=acc[:],
+                    lhsT=words.bitcast(FP8X4),
+                    lhsT_scale=scales,
+                    rhs=pick(wt, word_groups, e, 2 * H).bitcast(FP4X4),
+                    rhs_scale=pick(st, scale_groups, e, H),
+                    start=True,
+                    stop=True,
+                )
+            sig = ring.tile([P, H], F32, name="sig")
+            nc.scalar.activation(
+                sig[:].rearrange("s (u p v) -> s u p v", u=2, v=2),
+                a[:].rearrange("s (p u v) -> s u p v", u=2, v=2),
+                SIGMOID,
+            )
+            h = ring.tile([P, H], BF16, name="h", align_bytes=64)
+            nc.vector.tensor_tensor(
+                h[:].rearrange("s (u p v) -> s u p v", u=2, v=2),
+                b[:].rearrange("s (p u v) -> s u p v", u=2, v=2),
+                sig[:].rearrange("s (u p v) -> s u p v", u=2, v=2),
+                MULT,
+            )
+            hidden[j] = h
+
+        def turn(g, blocks):
+            n = len(blocks)
+            t = next_s()
+            for i, j in enumerate(blocks):
+                pairs = hidden[j][:].bitcast(F32)
+                for u in range(2):
+                    nc.tensor.transpose(
+                        t[:, (2 * i + u) * P : (2 * i + u + 1) * P], pairs[:, u * P : (u + 1) * P], ident[:]
+                    )
+            ht = ring.tile([P, 2 * BLOCK * 4], BF16, name="ht", align_bytes=64, bufs=2)
+            nc.scalar.copy(
+                ht[:, : n * BLOCK * 4].bitcast(F32).rearrange("p (i s u) -> p i s u", i=n, u=2),
+                t[:, : n * 2 * P].rearrange("p (i u s) -> p i s u", i=n, u=2),
+            )
+            cols = slice(blocks[0] * BLOCK, (blocks[-1] + 1) * BLOCK)
+            nc.vector.quantize_mx(out=hw[:, cols].bitcast(FP8X4), scales=hs[:, cols], in_=ht[:, : n * BLOCK * 4])
+
+        def second(acc, e, c0, c1):
+            nc.tensor.matmul_mx(
+                out=acc,
+                lhsT=w2[:, e * 2 * N : (e + 1) * 2 * N].bitcast(FP4X4),
+                lhsT_scale=s2[:, e * N : (e + 1) * N],
+                rhs=hw[:, c0:c1].bitcast(FP8X4),
+                rhs_scale=hs[:, c0:c1],
+                start=True,
+                stop=True,
+            )
+
+        def routed_out(blocks):
+            acc = next_s()
+            for i, j in enumerate(blocks):
+                second(acc[:, i * C : (i + 1) * C], j, j * C, (j + 1) * C)
+            a, b = blocks[0] * C, (blocks[-1] + 1) * C
+            nc.scalar.copy(y[:, a:b], acc[:, : b - a])
+
+        def scatter(a, b):
+            nc.vector.tensor_tensor(routed[:].indirect(offsets[:, a // 16 : b // 16]), y[:, a:b], gates[:, a:b], MULT)
+
+        def shared_out(a, b):
+            acc = next_s()
+            second(acc[:, : b - a], E, SLOTS + a, SLOTS + b)
+            res = keep.tile([P, b - a], F32, name="res%d" % a)
+            nc.vector.tensor_tensor(res[:], acc[:, : b - a], routed[:, a:b], ADD)
+            nc.sync.dma_start(out=out[:, a:b], in_=res[:])
+
+        groups = [(0, 1), (2, 3), (4, 5), (6, 7), (8, 9), (10, 11), (12, 13), (14,), (15,)]
+        ahead = 2
+        for g in range(ahead):
+            for j in groups[g]:
+                first(j)
+        pieces = [(0, 256), (256, 512), (512, 768)]
+        chunks = [512, 1024, 1152, 1280]
+        done = set()
+        done_at = {}
+        ready = 0
+        stored = 0
+        for g in range(len(groups) + 4):
+            if g + ahead < len(groups):
+                for j in groups[g + ahead]:
+                    first(j)
+            if g < len(groups):
+                turn(g, groups[g])
+                done = done | set(groups[g])
+            done_at[g] = done
+            if 0 <= g - 0 < len(groups) and groups[g - 0][0] < E:
+                routed_out(groups[g - 0])
+                ready = (groups[g - 0][-1] + 1) * C
+            while pieces and pieces[0][1] <= ready:
+                scatter(*pieces[0])
+                pieces = pieces[1:]
+            if not pieces:
+                for c in chunks:
+                    if c > stored and all(E + b in done_at.get(g - 1, set()) for b in range(c // BLOCK)):
+                        shared_out(stored, c)
+                        stored = c

@@ -35,63 +35,59 @@ def tile_moe_shr_glu_sigmoid_kernel(
 
         offsets = keep.tile([P, SLOTS // 16], U16, name="offsets")
         xw = keep.tile([P, T], I32, name="xw", align_bytes=64)
-        xs = keep.tile([P, T], U8, name="xs", align_bytes=64)
 
         def plane(name, width):
             t = keep.tile([P, width], U8, name=name, align_bytes=64)
             nc.vector.memset(t[:].bitcast(I32), 0)
             return t
 
-        def load_scales(t, src, e0, e1):
-            for r in range(4):
-                nc.sync.dma_start(
+        def load_scales(t, src, span, queue, rows):
+            e0, e1 = span
+            for r in rows:
+                queue.dma_start(
                     out=t[:].bitcast(I32)[r:P:32, :].rearrange("q (e n) -> q e n", e=e1 - e0),
                     in_=src[e0:e1, 0, r:16:4, :].rearrange("e q n -> q e n").bitcast(I32),
                 )
 
-        def load_words(name, src, e0, e1):
+        def load_words(name, src, span, queue=nc.sync):
+            e0, e1 = span
             width = src.shape[3]
             t = keep.tile([P, (e1 - e0) * width], U8, name=name, align_bytes=64)
-            nc.sync.dma_start(
+            queue.dma_start(
                 out=t[:].bitcast(I32).rearrange("p (e n) -> p e n", e=e1 - e0),
                 in_=src[e0:e1, 0, :, :].rearrange("e p n -> p e n").bitcast(I32),
             )
             return t
 
-        nc.vector.memset(xs[:].bitcast(I32), 0)
-        scale_groups = [(0, 3), (3, 7)]
-        word_groups = [(0, 2), (2, 4), (4, 7)]
-        s1 = [plane("s1_%d" % g, (e1 - e0) * H) for g, (e0, e1) in enumerate(scale_groups[:1])]
-        s3 = [plane("s3_%d" % g, (e1 - e0) * H) for g, (e0, e1) in enumerate(scale_groups[:1])]
-        s1 = s1 + [plane("s1_%d" % (g + 1), (e1 - e0) * H) for g, (e0, e1) in enumerate(scale_groups[1:])]
-        s3 = s3 + [plane("s3_%d" % (g + 1), (e1 - e0) * H) for g, (e0, e1) in enumerate(scale_groups[1:])]
+        scale_groups = [(4, 7), (0, 4)]
+        word_groups = [(4, 7), (0, 4)]
+        s3 = [plane("s3_0", 3 * H)]
+        xs = plane("xs", T)
+        s1 = [plane("s1_0", 3 * H)]
         s2 = plane("s2", (E + 1) * N)
+        s1.append(plane("s1_1", 4 * H))
+        s3.append(plane("s3_1", 4 * H))
         routed = keep.tile([P, T], F32, name="routed")
         nc.vector.memset(routed[:], 0.0)
+        gates = keep.tile([P, SLOTS], F32, name="gates")
+        load_scales(s3[0], w3_scales, scale_groups[0], nc.gpsimd, [2, 3])
         ident = keep.tile([P, P], F32, name="ident")
         make_identity(nc, ident[:])
-        warm = keep.tile([P, 8], F32, name="warm")
-        nc.scalar.activation(warm[:], ident[:, 0:8], SIGMOID)
+        load_scales(s2, w2_scales, (0, E + 1), nc.gpsimd, range(4))
 
         nc.sync.dma_start(out=xw[:], in_=x_words[0].rearrange("p t r -> p (t r)").bitcast(I32))
-        nc.sync.dma_start(offsets[:], offs)
         for r in range(4):
             nc.sync.dma_start(out=xs[:].bitcast(I32)[r:P:32, :], in_=x_scales[0, r:16:4, :].bitcast(I32))
-        w1 = [load_words("w1_0", w1_words, *word_groups[0])]
-        w3 = [load_words("w3_0", w3_words, *word_groups[0])]
-        load_scales(s1[0], w1_scales, *scale_groups[0])
-        load_scales(s3[0], w3_scales, *scale_groups[0])
-        w1.append(load_words("w1_1", w1_words, *word_groups[1]))
-        w3.append(load_words("w3_1", w3_words, *word_groups[1]))
-        for g in range(1, len(scale_groups)):
-            load_scales(s1[g], w1_scales, *scale_groups[g])
-            load_scales(s3[g], w3_scales, *scale_groups[g])
-        w2 = load_words("w2", w2_words, 0, E + 1)
-        load_scales(s2, w2_scales, 0, E + 1)
-        for g in range(2, len(word_groups)):
-            w1.append(load_words("w1_%d" % g, w1_words, *word_groups[g]))
-            w3.append(load_words("w3_%d" % g, w3_words, *word_groups[g]))
-        gates = keep.tile([P, SLOTS], F32, name="gates")
+        nc.sync.dma_start(offsets[:], offs)
+        w1 = [load_words("w1_0", w1_words, word_groups[0])]
+        w3 = [load_words("w3_0", w3_words, word_groups[0])]
+        load_scales(s1[0], w1_scales, scale_groups[0], nc.sync, range(4))
+        load_scales(s3[0], w3_scales, scale_groups[0], nc.sync, [0, 1])
+        load_scales(s1[1], w1_scales, scale_groups[1], nc.sync, range(4))
+        load_scales(s3[1], w3_scales, scale_groups[1], nc.sync, range(4))
+        w1.append(load_words("w1_1", w1_words, word_groups[1]))
+        w3.append(load_words("w3_1", w3_words, word_groups[1]))
+        w2 = load_words("w2", w2_words, (0, E + 1))
         nc.sync.dma_start(out=gates[:], in_=gate)
 
         def pick(tiles, groups, e, width):
@@ -99,7 +95,7 @@ def tile_moe_shr_glu_sigmoid_kernel(
                 if e0 <= e < e1:
                     return t[:, (e - e0) * width : (e - e0 + 1) * width]
 
-        cuts = [(0, 256), (256, 768)]
+        cuts = [(512, 768), (0, 512)]
         gw, gs = [], []
         for g, (a, b) in enumerate(cuts):
             tw = keep.tile([P, b - a], U32, name="gw%d" % g, align_bytes=64)
@@ -109,19 +105,17 @@ def tile_moe_shr_glu_sigmoid_kernel(
             gw.append(tw)
             gs.append(ts)
 
-        ring_s = [psum.tile([P, BANK], F32, name="s%d" % i) for i in range(5)]
-        bank_b = [psum.tile([P, BANK], F32, name="b%d" % i) for i in range(3)]
-        taken = []
+        ring_s = [psum.tile([P, BANK], F32, name="s%d" % i) for i in range(3)]
+        ring_b = [psum.tile([P, BANK], F32, name="b%d" % i) for i in range(5)]
+        taken_s, taken_b = [], []
 
         def next_s():
-            taken.append(0)
-            return ring_s[len(taken) % len(ring_s)]
-
-        begun = []
+            taken_s.append(0)
+            return ring_s[len(taken_s) % len(ring_s)]
 
         def next_b():
-            begun.append(0)
-            return bank_b[len(begun) % len(bank_b)]
+            taken_b.append(0)
+            return ring_b[len(taken_b) % len(ring_b)]
 
         hw = keep.tile([P, SLOTS + T], U32, name="hw", align_bytes=64)
         hs = keep.tile([P, SLOTS + T], U8, name="hs", align_bytes=64)
@@ -167,7 +161,7 @@ def tile_moe_shr_glu_sigmoid_kernel(
             )
             hidden[j] = h
 
-        def turn(g, blocks):
+        def turn(blocks):
             n = len(blocks)
             t = next_s()
             for i, j in enumerate(blocks):
@@ -176,7 +170,7 @@ def tile_moe_shr_glu_sigmoid_kernel(
                     nc.tensor.transpose(
                         t[:, (2 * i + u) * P : (2 * i + u + 1) * P], pairs[:, u * P : (u + 1) * P], ident[:]
                     )
-            ht = ring.tile([P, 2 * BLOCK * 4], BF16, name="ht", align_bytes=64, bufs=2)
+            ht = ring.tile([P, 2 * BLOCK * 4], BF16, name="ht", align_bytes=64, bufs=4)
             nc.scalar.copy(
                 ht[:, : n * BLOCK * 4].bitcast(F32).rearrange("p (i s u) -> p i s u", i=n, u=2),
                 t[:, : n * 2 * P].rearrange("p (i u s) -> p i s u", i=n, u=2),
@@ -196,49 +190,42 @@ def tile_moe_shr_glu_sigmoid_kernel(
             )
 
         def routed_out(blocks):
-            acc = next_s()
+            acc = next_b()
             for i, j in enumerate(blocks):
                 second(acc[:, i * C : (i + 1) * C], j, j * C, (j + 1) * C)
             a, b = blocks[0] * C, (blocks[-1] + 1) * C
             nc.scalar.copy(y[:, a:b], acc[:, : b - a])
-
-        def scatter(a, b):
             nc.vector.tensor_tensor(routed[:].indirect(offsets[:, a // 16 : b // 16]), y[:, a:b], gates[:, a:b], MULT)
 
         def shared_out(a, b):
-            acc = next_s()
+            acc = next_b()
             second(acc[:, : b - a], E, SLOTS + a, SLOTS + b)
             res = keep.tile([P, b - a], F32, name="res%d" % a)
             nc.vector.tensor_tensor(res[:], acc[:, : b - a], routed[:, a:b], ADD)
             nc.sync.dma_start(out=out[:, a:b], in_=res[:])
 
-        groups = [(0, 1), (2, 3), (4, 5), (6, 7), (8, 9), (10, 11), (12, 13), (14,), (15,)]
+        groups = [(4, 5), (6, 7), (8, 9), (10, 11), (0, 1), (2, 3), (12, 13), (14, 15)]
         ahead = 2
+        lag = 2
+        chunks = [512, 1024, 1280]
         for g in range(ahead):
             for j in groups[g]:
                 first(j)
-        pieces = [(0, 256), (256, 512), (512, 768)]
-        chunks = [512, 1024, 1152, 1280]
         done = set()
-        done_at = {}
-        ready = 0
+        scattered = 0
         stored = 0
-        for g in range(len(groups) + 4):
+        for g in range(len(groups) + lag):
             if g + ahead < len(groups):
                 for j in groups[g + ahead]:
                     first(j)
             if g < len(groups):
-                turn(g, groups[g])
+                turn(groups[g])
                 done = done | set(groups[g])
-            done_at[g] = done
-            if 0 <= g - 0 < len(groups) and groups[g - 0][0] < E:
-                routed_out(groups[g - 0])
-                ready = (groups[g - 0][-1] + 1) * C
-            while pieces and pieces[0][1] <= ready:
-                scatter(*pieces[0])
-                pieces = pieces[1:]
-            if not pieces:
+            if 0 <= g - lag and groups[g - lag][0] < E:
+                routed_out(groups[g - lag])
+                scattered = scattered + len(groups[g - lag])
+            if scattered == E:
                 for c in chunks:
-                    if c > stored and all(E + b in done_at.get(g - 1, set()) for b in range(c // BLOCK)):
+                    if c > stored and all(E + b in done for b in range(c // BLOCK)):
                         shared_out(stored, c)
                         stored = c

@@ -64,16 +64,15 @@ def tile_moe_shr_glu_sigmoid_kernel(
         s3 = [plane("s3_0", 3 * H)]
         xs = plane("xs", T)
         s1 = [plane("s1_0", 3 * H)]
-        s2 = plane("s2", (E + 1) * N)
         s1.append(plane("s1_1", 4 * H))
         s3.append(plane("s3_1", 4 * H))
+        s2 = plane("s2", (E + 1) * N)
         routed = keep.tile([P, T], F32, name="routed")
         nc.vector.memset(routed[:], 0.0)
         gates = keep.tile([P, SLOTS], F32, name="gates")
         load_scales(s3[0], w3_scales, scale_groups[0], nc.gpsimd, [2, 3])
         ident = keep.tile([P, P], F32, name="ident")
         make_identity(nc, ident[:])
-        load_scales(s2, w2_scales, (0, E + 1), nc.gpsimd, range(4))
 
         nc.sync.dma_start(out=xw[:], in_=x_words[0].rearrange("p t r -> p (t r)").bitcast(I32))
         for r in range(4):
@@ -88,6 +87,7 @@ def tile_moe_shr_glu_sigmoid_kernel(
         w1.append(load_words("w1_1", w1_words, word_groups[1]))
         w3.append(load_words("w3_1", w3_words, word_groups[1]))
         w2 = load_words("w2", w2_words, (0, E + 1))
+        load_scales(s2, w2_scales, (0, E + 1), nc.sync, range(4))
         nc.sync.dma_start(out=gates[:], in_=gate)
 
         def pick(tiles, groups, e, width):

@@ -22,6 +22,27 @@ SIGMOID = mybir.ActivationFunctionType.Sigmoid
 P = 128
 BLOCK = 128
 BANK = 512
+LIST_ROWS = 16
+SCALE_ROWS = 16
+ROWS_A_QUADRANT = 4
+
+EARLY = (E - 2, E + 1)
+LATE = (0, E - 2)
+
+ROUTED_PAIRS = [(j, j + 1) for j in range(0, E, 2)]
+SHARED_PAIRS = [(j, j + 1) for j in range(E, E + T // BLOCK, 2)]
+SHARED_PAIRS_BEFORE_LATE = 3
+PAIRS = (
+    ROUTED_PAIRS[-1:] + SHARED_PAIRS[:SHARED_PAIRS_BEFORE_LATE] + ROUTED_PAIRS[:-1] + SHARED_PAIRS[SHARED_PAIRS_BEFORE_LATE:]
+)
+AHEAD = 2
+LAG = 2
+
+SCALAR_BANKS = 3
+HELD_BANKS = 5
+STREAM_BUFS = 6
+TURNED_BUFS = 4
+WARM_UP_PASSES = 2
 
 
 def tile_moe_shr_glu_sigmoid_kernel(
@@ -30,202 +51,192 @@ def tile_moe_shr_glu_sigmoid_kernel(
     nc = tc.nc
     with ExitStack() as ctx:
         keep = ctx.enter_context(tc.tile_pool(name="keep", bufs=1))
-        ring = ctx.enter_context(tc.tile_pool(name="ring", bufs=6))
+        ring = ctx.enter_context(tc.tile_pool(name="ring", bufs=STREAM_BUFS))
         psum = ctx.enter_context(tc.psum_pool(name="psum", bufs=1))
 
-        offsets = keep.tile([P, SLOTS // 16], U16, name="offsets")
+        offsets = keep.tile([P, SLOTS // LIST_ROWS], U16, name="offsets")
         xw = keep.tile([P, T], I32, name="xw", align_bytes=64)
 
         def plane(name, width):
-            t = keep.tile([P, width], U8, name=name, align_bytes=64)
-            nc.vector.memset(t[:].bitcast(I32), 0)
-            return t
+            tile = keep.tile([P, width], U8, name=name, align_bytes=64)
+            nc.vector.memset(tile[:].bitcast(I32), 0)
+            return tile
 
-        def load_scales(t, src, span, queue, rows):
-            e0, e1 = span
+        def load_scales(tile, src, experts, queue, rows):
+            e0, e1 = experts
             for r in rows:
                 queue.dma_start(
-                    out=t[:].bitcast(I32)[r:P:32, :].rearrange("q (e n) -> q e n", e=e1 - e0),
-                    in_=src[e0:e1, 0, r:16:4, :].rearrange("e q n -> q e n").bitcast(I32),
+                    out=tile[:].bitcast(I32)[r:P:32, :].rearrange("q (e n) -> q e n", e=e1 - e0),
+                    in_=src[e0:e1, 0, r:SCALE_ROWS:ROWS_A_QUADRANT, :].rearrange("e q n -> q e n").bitcast(I32),
                 )
 
-        def load_words(name, src, span, queue=nc.sync):
-            e0, e1 = span
-            width = src.shape[3]
-            t = keep.tile([P, (e1 - e0) * width], U8, name=name, align_bytes=64)
-            queue.dma_start(
-                out=t[:].bitcast(I32).rearrange("p (e n) -> p e n", e=e1 - e0),
+        def load_words(name, src, experts):
+            e0, e1 = experts
+            tile = keep.tile([P, (e1 - e0) * src.shape[3]], U8, name=name, align_bytes=64)
+            nc.sync.dma_start(
+                out=tile[:].bitcast(I32).rearrange("p (e n) -> p e n", e=e1 - e0),
                 in_=src[e0:e1, 0, :, :].rearrange("e p n -> p e n").bitcast(I32),
             )
-            return t
+            return tile
 
-        scale_groups = [(4, 7), (0, 4)]
-        word_groups = [(4, 7), (0, 4)]
-        s3 = [plane("s3_0", 3 * H)]
+        all_rows = range(ROWS_A_QUADRANT)
+        all_experts = (0, E + 1)
+        s3 = {EARLY: plane("s3_0", (EARLY[1] - EARLY[0]) * H)}
         xs = plane("xs", T)
-        s1 = [plane("s1_0", 3 * H)]
-        s1.append(plane("s1_1", 4 * H))
-        s3.append(plane("s3_1", 4 * H))
+        s1 = {EARLY: plane("s1_0", (EARLY[1] - EARLY[0]) * H)}
+        s1[LATE] = plane("s1_1", (LATE[1] - LATE[0]) * H)
+        s3[LATE] = plane("s3_1", (LATE[1] - LATE[0]) * H)
         s2 = plane("s2", (E + 1) * N)
         routed = keep.tile([P, T], F32, name="routed")
         nc.vector.memset(routed[:], 0.0)
         gates = keep.tile([P, SLOTS], F32, name="gates")
-        load_scales(s3[0], w3_scales, scale_groups[0], nc.gpsimd, [2, 3])
+
+        load_scales(s3[EARLY], w3_scales, EARLY, nc.gpsimd, all_rows[2:])
         ident = keep.tile([P, P], F32, name="ident")
         make_identity(nc, ident[:])
 
         nc.sync.dma_start(out=xw[:], in_=x_words[0].rearrange("p t r -> p (t r)").bitcast(I32))
-        for r in range(4):
-            nc.sync.dma_start(out=xs[:].bitcast(I32)[r:P:32, :], in_=x_scales[0, r:16:4, :].bitcast(I32))
+        for r in all_rows:
+            nc.sync.dma_start(
+                out=xs[:].bitcast(I32)[r:P:32, :], in_=x_scales[0, r:SCALE_ROWS:ROWS_A_QUADRANT, :].bitcast(I32)
+            )
         nc.sync.dma_start(offsets[:], offs)
-        w1 = [load_words("w1_0", w1_words, word_groups[0])]
-        w3 = [load_words("w3_0", w3_words, word_groups[0])]
-        load_scales(s1[0], w1_scales, scale_groups[0], nc.sync, range(4))
-        load_scales(s3[0], w3_scales, scale_groups[0], nc.sync, [0, 1])
-        load_scales(s1[1], w1_scales, scale_groups[1], nc.sync, range(4))
-        load_scales(s3[1], w3_scales, scale_groups[1], nc.sync, range(4))
-        w1.append(load_words("w1_1", w1_words, word_groups[1]))
-        w3.append(load_words("w3_1", w3_words, word_groups[1]))
-        w2 = load_words("w2", w2_words, (0, E + 1))
-        load_scales(s2, w2_scales, (0, E + 1), nc.sync, range(4))
+        w1 = {EARLY: load_words("w1_0", w1_words, EARLY)}
+        w3 = {EARLY: load_words("w3_0", w3_words, EARLY)}
+        load_scales(s1[EARLY], w1_scales, EARLY, nc.sync, all_rows)
+        load_scales(s3[EARLY], w3_scales, EARLY, nc.sync, all_rows[:2])
+        load_scales(s1[LATE], w1_scales, LATE, nc.sync, all_rows)
+        load_scales(s3[LATE], w3_scales, LATE, nc.sync, all_rows)
+        w1[LATE] = load_words("w1_1", w1_words, LATE)
+        w3[LATE] = load_words("w3_1", w3_words, LATE)
+        w2 = load_words("w2", w2_words, all_experts)
+        load_scales(s2, w2_scales, all_experts, nc.sync, all_rows)
         nc.sync.dma_start(out=gates[:], in_=gate)
 
-        def pick(tiles, groups, e, width):
-            for t, (e0, e1) in zip(tiles, groups):
-                if e0 <= e < e1:
-                    return t[:, (e - e0) * width : (e - e0 + 1) * width]
+        def of_expert(tiles, e, width):
+            experts = EARLY if e >= EARLY[0] else LATE
+            return tiles[experts][:, (e - experts[0]) * width : (e - experts[0] + 1) * width]
 
-        cuts = [(512, 768), (0, 512)]
-        gw, gs = [], []
-        for g, (a, b) in enumerate(cuts):
-            tw = keep.tile([P, b - a], U32, name="gw%d" % g, align_bytes=64)
-            ts = keep.tile([P, b - a], U8, name="gs%d" % g, align_bytes=64)
-            nc.vector.tensor_copy(tw[:], xw[:].bitcast(U32).indirect(offsets[:, a // 16 : b // 16]))
-            nc.vector.tensor_copy(ts[:], xs[:].indirect(offsets[:, a // 16 : b // 16]))
-            gw.append(tw)
-            gs.append(ts)
+        def list_slice(lo, hi):
+            return offsets[:, lo // LIST_ROWS : hi // LIST_ROWS]
 
-        ring_s = [psum.tile([P, BANK], F32, name="s%d" % i) for i in range(3)]
-        ring_b = [psum.tile([P, BANK], F32, name="b%d" % i) for i in range(5)]
-        taken_s, taken_b = [], []
+        gathered = {}
+        for part, (lo, hi) in enumerate([(EARLY[0] * C, SLOTS), (0, EARLY[0] * C)]):
+            slot_words = keep.tile([P, hi - lo], U32, name="gw%d" % part, align_bytes=64)
+            slot_scales = keep.tile([P, hi - lo], U8, name="gs%d" % part, align_bytes=64)
+            nc.vector.tensor_copy(slot_words[:], xw[:].bitcast(U32).indirect(list_slice(lo, hi)))
+            nc.vector.tensor_copy(slot_scales[:], xs[:].indirect(list_slice(lo, hi)))
+            for e in range(lo // C, hi // C):
+                cols = slice(e * C - lo, (e + 1) * C - lo)
+                gathered[e] = (slot_words[:, cols], slot_scales[:, cols])
 
-        def next_s():
-            taken_s.append(0)
-            return ring_s[len(taken_s) % len(ring_s)]
+        scalar_banks = [psum.tile([P, BANK], F32, name="s%d" % bank) for bank in range(SCALAR_BANKS)]
+        held_banks = [psum.tile([P, BANK], F32, name="b%d" % bank) for bank in range(HELD_BANKS)]
 
-        def next_b():
-            taken_b.append(0)
-            return ring_b[len(taken_b) % len(ring_b)]
+        def take(banks):
+            banks.append(banks.pop(0))
+            return banks[0]
+
+        for bank in range(WARM_UP_PASSES):
+            nc.tensor.matmul_mx(
+                out=held_banks[-1 - bank][:],
+                lhsT=xw[:, :BLOCK].bitcast(FP8X4),
+                lhsT_scale=xs[:, :BLOCK],
+                rhs=w1[EARLY][:, : 2 * H].bitcast(FP4X4),
+                rhs_scale=xs[:, :H],
+                start=True,
+                stop=True,
+            )
 
         hw = keep.tile([P, SLOTS + T], U32, name="hw", align_bytes=64)
         hs = keep.tile([P, SLOTS + T], U8, name="hs", align_bytes=64)
         y = keep.tile([P, SLOTS], F32, name="y")
-
-        def operand(j):
-            if j < E:
-                for tw, ts, (a, b) in zip(gw, gs, cuts):
-                    if a <= j * C < b:
-                        cols = slice(j * C - a, (j + 1) * C - a)
-                        return tw[:, cols], ts[:, cols], j
-            cols = slice((j - E) * BLOCK, (j - E + 1) * BLOCK)
-            return xw[:, cols], xs[:, cols], E
-
         hidden = {}
 
-        def first(j):
-            words, scales, e = operand(j)
-            a = next_s()
-            b = next_b()
-            for acc, wt, st in ((a, w1, s1), (b, w3, s3)):
+        def first_products(j):
+            if j < E:
+                words, scales = gathered[j]
+            else:
+                cols = slice((j - E) * BLOCK, (j - E + 1) * BLOCK)
+                words, scales = xw[:, cols], xs[:, cols]
+            e = min(j, E)
+            acc1 = take(scalar_banks)
+            acc3 = take(held_banks)
+            for acc, w_words, w_scales in ((acc1, w1, s1), (acc3, w3, s3)):
                 nc.tensor.matmul_mx(
                     out=acc[:],
                     lhsT=words.bitcast(FP8X4),
                     lhsT_scale=scales,
-                    rhs=pick(wt, word_groups, e, 2 * H).bitcast(FP4X4),
-                    rhs_scale=pick(st, scale_groups, e, H),
+                    rhs=of_expert(w_words, e, 2 * H).bitcast(FP4X4),
+                    rhs_scale=of_expert(w_scales, e, H),
                     start=True,
                     stop=True,
                 )
             sig = ring.tile([P, H], F32, name="sig")
             nc.scalar.activation(
                 sig[:].rearrange("s (u p v) -> s u p v", u=2, v=2),
-                a[:].rearrange("s (p u v) -> s u p v", u=2, v=2),
+                acc1[:].rearrange("s (p u v) -> s u p v", u=2, v=2),
                 SIGMOID,
             )
             h = ring.tile([P, H], BF16, name="h", align_bytes=64)
             nc.vector.tensor_tensor(
                 h[:].rearrange("s (u p v) -> s u p v", u=2, v=2),
-                b[:].rearrange("s (p u v) -> s u p v", u=2, v=2),
+                acc3[:].rearrange("s (p u v) -> s u p v", u=2, v=2),
                 sig[:].rearrange("s (u p v) -> s u p v", u=2, v=2),
                 MULT,
             )
             hidden[j] = h
 
-        def turn(blocks):
-            n = len(blocks)
-            t = next_s()
-            for i, j in enumerate(blocks):
-                pairs = hidden[j][:].bitcast(F32)
+        def turn_and_quantise(pair):
+            turned = take(scalar_banks)
+            for side, j in enumerate(pair):
+                value_pairs = hidden[j][:].bitcast(F32)
                 for u in range(2):
-                    nc.tensor.transpose(
-                        t[:, (2 * i + u) * P : (2 * i + u + 1) * P], pairs[:, u * P : (u + 1) * P], ident[:]
-                    )
-            ht = ring.tile([P, 2 * BLOCK * 4], BF16, name="ht", align_bytes=64, bufs=4)
+                    at = (2 * side + u) * P
+                    nc.tensor.transpose(turned[:, at : at + P], value_pairs[:, u * P : (u + 1) * P], ident[:])
+            ht = ring.tile([P, 2 * BLOCK * 4], BF16, name="ht", align_bytes=64, bufs=TURNED_BUFS)
             nc.scalar.copy(
-                ht[:, : n * BLOCK * 4].bitcast(F32).rearrange("p (i s u) -> p i s u", i=n, u=2),
-                t[:, : n * 2 * P].rearrange("p (i u s) -> p i s u", i=n, u=2),
+                ht[:].bitcast(F32).rearrange("p (side s u) -> p side s u", side=2, u=2),
+                turned[:].rearrange("p (side u s) -> p side s u", side=2, u=2),
             )
-            cols = slice(blocks[0] * BLOCK, (blocks[-1] + 1) * BLOCK)
-            nc.vector.quantize_mx(out=hw[:, cols].bitcast(FP8X4), scales=hs[:, cols], in_=ht[:, : n * BLOCK * 4])
+            cols = slice(pair[0] * BLOCK, (pair[1] + 1) * BLOCK)
+            nc.vector.quantize_mx(out=hw[:, cols].bitcast(FP8X4), scales=hs[:, cols], in_=ht[:])
 
-        def second(acc, e, c0, c1):
+        def second_product(acc, e, lo, hi):
             nc.tensor.matmul_mx(
                 out=acc,
                 lhsT=w2[:, e * 2 * N : (e + 1) * 2 * N].bitcast(FP4X4),
                 lhsT_scale=s2[:, e * N : (e + 1) * N],
-                rhs=hw[:, c0:c1].bitcast(FP8X4),
-                rhs_scale=hs[:, c0:c1],
+                rhs=hw[:, lo:hi].bitcast(FP8X4),
+                rhs_scale=hs[:, lo:hi],
                 start=True,
                 stop=True,
             )
 
-        def routed_out(blocks):
-            acc = next_b()
-            for i, j in enumerate(blocks):
-                second(acc[:, i * C : (i + 1) * C], j, j * C, (j + 1) * C)
-            a, b = blocks[0] * C, (blocks[-1] + 1) * C
-            nc.scalar.copy(y[:, a:b], acc[:, : b - a])
-            nc.vector.tensor_tensor(routed[:].indirect(offsets[:, a // 16 : b // 16]), y[:, a:b], gates[:, a:b], MULT)
+        def scatter_routed(pair):
+            acc = take(held_banks)
+            for side, e in enumerate(pair):
+                second_product(acc[:, side * C : (side + 1) * C], e, e * C, (e + 1) * C)
+            lo, hi = pair[0] * C, (pair[1] + 1) * C
+            nc.scalar.copy(y[:, lo:hi], acc[:, : hi - lo])
+            nc.vector.tensor_tensor(routed[:].indirect(list_slice(lo, hi)), y[:, lo:hi], gates[:, lo:hi], MULT)
 
-        def shared_out(a, b):
-            acc = next_b()
-            second(acc[:, : b - a], E, SLOTS + a, SLOTS + b)
-            res = keep.tile([P, b - a], F32, name="res%d" % a)
-            nc.vector.tensor_tensor(res[:], acc[:, : b - a], routed[:, a:b], ADD)
-            nc.sync.dma_start(out=out[:, a:b], in_=res[:])
+        def add_shared_and_store(lo, hi):
+            acc = take(held_banks)
+            second_product(acc[:, : hi - lo], E, SLOTS + lo, SLOTS + hi)
+            res = keep.tile([P, hi - lo], F32, name="res%d" % lo)
+            nc.vector.tensor_tensor(res[:], acc[:, : hi - lo], routed[:, lo:hi], ADD)
+            nc.sync.dma_start(out=out[:, lo:hi], in_=res[:])
 
-        groups = [(4, 5), (6, 7), (8, 9), (10, 11), (0, 1), (2, 3), (12, 13), (14, 15)]
-        ahead = 2
-        lag = 2
-        chunks = [512, 1024, 1280]
-        for g in range(ahead):
-            for j in groups[g]:
-                first(j)
-        done = set()
-        scattered = 0
-        stored = 0
-        for g in range(len(groups) + lag):
-            if g + ahead < len(groups):
-                for j in groups[g + ahead]:
-                    first(j)
-            if g < len(groups):
-                turn(groups[g])
-                done = done | set(groups[g])
-            if 0 <= g - lag and groups[g - lag][0] < E:
-                routed_out(groups[g - lag])
-                scattered = scattered + len(groups[g - lag])
-            if scattered == E:
-                for c in chunks:
-                    if c > stored and all(E + b in done for b in range(c // BLOCK)):
-                        shared_out(stored, c)
-                        stored = c
+        for pair in PAIRS[:AHEAD]:
+            for j in pair:
+                first_products(j)
+        for step, pair in enumerate(PAIRS):
+            if step + AHEAD < len(PAIRS):
+                for j in PAIRS[step + AHEAD]:
+                    first_products(j)
+            turn_and_quantise(pair)
+            if step >= LAG and PAIRS[step - LAG] in ROUTED_PAIRS:
+                scatter_routed(PAIRS[step - LAG])
+        for lo in range(0, T, BANK):
+            add_shared_and_store(lo, min(lo + BANK, T))

from contextlib import ExitStack

import concourse.mybir as mybir
from concourse.masks import make_identity

K, T, E, C, H, N = 512, 1280, 6, 128, 512, 128
SLOTS = E * C
FLOPS = 2 * (SLOTS + T) * (2 * K * H + H * N)

F32 = mybir.dt.float32
BF16 = mybir.dt.bfloat16
I32 = mybir.dt.int32
U32 = mybir.dt.uint32
U16 = mybir.dt.uint16
U8 = mybir.dt.uint8
FP8X4 = mybir.dt.float8_e4m3fn_x4
FP4X4 = mybir.dt.float4_e2m1fn_x4
MULT = mybir.AluOpType.mult
ADD = mybir.AluOpType.add
SIGMOID = mybir.ActivationFunctionType.Sigmoid

P = 128
BLOCK = 128
BANK = 512
LIST_ROWS = 16
SCALE_ROWS = 16
ROWS_A_QUADRANT = 4

EARLY = (E - 2, E + 1)
LATE = (0, E - 2)

ROUTED_PAIRS = [(j, j + 1) for j in range(0, E, 2)]
SHARED_PAIRS = [(j, j + 1) for j in range(E, E + T // BLOCK, 2)]
SHARED_PAIRS_BEFORE_LATE = 3
PAIRS = (
    ROUTED_PAIRS[-1:] + SHARED_PAIRS[:SHARED_PAIRS_BEFORE_LATE] + ROUTED_PAIRS[:-1] + SHARED_PAIRS[SHARED_PAIRS_BEFORE_LATE:]
)
AHEAD = 2
LAG = 2

SCALAR_BANKS = 3
HELD_BANKS = 5
STREAM_BUFS = 6
TURNED_BUFS = 4
WARM_UP_PASSES = 2


def tile_moe_shr_glu_sigmoid_kernel(
    tc, x_words, x_scales, w1_words, w1_scales, w3_words, w3_scales, w2_words, w2_scales, gate, offs, out
):
    nc = tc.nc
    with ExitStack() as ctx:
        keep = ctx.enter_context(tc.tile_pool(name="keep", bufs=1))
        ring = ctx.enter_context(tc.tile_pool(name="ring", bufs=STREAM_BUFS))
        psum = ctx.enter_context(tc.psum_pool(name="psum", bufs=1))

        offsets = keep.tile([P, SLOTS // LIST_ROWS], U16, name="offsets")
        xw = keep.tile([P, T], I32, name="xw", align_bytes=64)

        def plane(name, width):
            tile = keep.tile([P, width], U8, name=name, align_bytes=64)
            nc.vector.memset(tile[:].bitcast(I32), 0)
            return tile

        def load_scales(tile, src, experts, queue, rows):
            e0, e1 = experts
            for r in rows:
                queue.dma_start(
                    out=tile[:].bitcast(I32)[r:P:32, :].rearrange("q (e n) -> q e n", e=e1 - e0),
                    in_=src[e0:e1, 0, r:SCALE_ROWS:ROWS_A_QUADRANT, :].rearrange("e q n -> q e n").bitcast(I32),
                )

        def load_words(name, src, experts):
            e0, e1 = experts
            tile = keep.tile([P, (e1 - e0) * src.shape[3]], U8, name=name, align_bytes=64)
            nc.sync.dma_start(
                out=tile[:].bitcast(I32).rearrange("p (e n) -> p e n", e=e1 - e0),
                in_=src[e0:e1, 0, :, :].rearrange("e p n -> p e n").bitcast(I32),
            )
            return tile

        all_rows = range(ROWS_A_QUADRANT)
        all_experts = (0, E + 1)
        s3 = {EARLY: plane("s3_0", (EARLY[1] - EARLY[0]) * H)}
        xs = plane("xs", T)
        s1 = {EARLY: plane("s1_0", (EARLY[1] - EARLY[0]) * H)}
        s1[LATE] = plane("s1_1", (LATE[1] - LATE[0]) * H)
        s3[LATE] = plane("s3_1", (LATE[1] - LATE[0]) * H)
        s2 = plane("s2", (E + 1) * N)
        routed = keep.tile([P, T], F32, name="routed")
        nc.vector.memset(routed[:], 0.0)
        gates = keep.tile([P, SLOTS], F32, name="gates")

        load_scales(s3[EARLY], w3_scales, EARLY, nc.gpsimd, all_rows[2:])
        ident = keep.tile([P, P], F32, name="ident")
        make_identity(nc, ident[:])

        nc.sync.dma_start(out=xw[:], in_=x_words[0].rearrange("p t r -> p (t r)").bitcast(I32))
        for r in all_rows:
            nc.sync.dma_start(
                out=xs[:].bitcast(I32)[r:P:32, :], in_=x_scales[0, r:SCALE_ROWS:ROWS_A_QUADRANT, :].bitcast(I32)
            )
        nc.sync.dma_start(offsets[:], offs)
        w1 = {EARLY: load_words("w1_0", w1_words, EARLY)}
        w3 = {EARLY: load_words("w3_0", w3_words, EARLY)}
        load_scales(s1[EARLY], w1_scales, EARLY, nc.sync, all_rows)
        load_scales(s3[EARLY], w3_scales, EARLY, nc.sync, all_rows[:2])
        load_scales(s1[LATE], w1_scales, LATE, nc.sync, all_rows)
        load_scales(s3[LATE], w3_scales, LATE, nc.sync, all_rows)
        w1[LATE] = load_words("w1_1", w1_words, LATE)
        w3[LATE] = load_words("w3_1", w3_words, LATE)
        w2 = load_words("w2", w2_words, all_experts)
        load_scales(s2, w2_scales, all_experts, nc.sync, all_rows)
        nc.sync.dma_start(out=gates[:], in_=gate)

        def of_expert(tiles, e, width):
            experts = EARLY if e >= EARLY[0] else LATE
            return tiles[experts][:, (e - experts[0]) * width : (e - experts[0] + 1) * width]

        def list_slice(lo, hi):
            return offsets[:, lo // LIST_ROWS : hi // LIST_ROWS]

        gathered = {}
        for part, (lo, hi) in enumerate([(EARLY[0] * C, SLOTS), (0, EARLY[0] * C)]):
            slot_words = keep.tile([P, hi - lo], U32, name="gw%d" % part, align_bytes=64)
            slot_scales = keep.tile([P, hi - lo], U8, name="gs%d" % part, align_bytes=64)
            nc.vector.tensor_copy(slot_words[:], xw[:].bitcast(U32).indirect(list_slice(lo, hi)))
            nc.vector.tensor_copy(slot_scales[:], xs[:].indirect(list_slice(lo, hi)))
            for e in range(lo // C, hi // C):
                cols = slice(e * C - lo, (e + 1) * C - lo)
                gathered[e] = (slot_words[:, cols], slot_scales[:, cols])

        scalar_banks = [psum.tile([P, BANK], F32, name="s%d" % bank) for bank in range(SCALAR_BANKS)]
        held_banks = [psum.tile([P, BANK], F32, name="b%d" % bank) for bank in range(HELD_BANKS)]

        def take(banks):
            banks.append(banks.pop(0))
            return banks[0]

        for bank in range(WARM_UP_PASSES):
            nc.tensor.matmul_mx(
                out=held_banks[-1 - bank][:],
                lhsT=xw[:, :BLOCK].bitcast(FP8X4),
                lhsT_scale=xs[:, :BLOCK],
                rhs=w1[EARLY][:, : 2 * H].bitcast(FP4X4),
                rhs_scale=xs[:, :H],
                start=True,
                stop=True,
            )

        hw = keep.tile([P, SLOTS + T], U32, name="hw", align_bytes=64)
        hs = keep.tile([P, SLOTS + T], U8, name="hs", align_bytes=64)
        y = keep.tile([P, SLOTS], F32, name="y")
        hidden = {}

        def first_products(j):
            if j < E:
                words, scales = gathered[j]
            else:
                cols = slice((j - E) * BLOCK, (j - E + 1) * BLOCK)
                words, scales = xw[:, cols], xs[:, cols]
            e = min(j, E)
            acc1 = take(scalar_banks)
            acc3 = take(held_banks)
            for acc, w_words, w_scales in ((acc1, w1, s1), (acc3, w3, s3)):
                nc.tensor.matmul_mx(
                    out=acc[:],
                    lhsT=words.bitcast(FP8X4),
                    lhsT_scale=scales,
                    rhs=of_expert(w_words, e, 2 * H).bitcast(FP4X4),
                    rhs_scale=of_expert(w_scales, e, H),
                    start=True,
                    stop=True,
                )
            sig = ring.tile([P, H], F32, name="sig")
            nc.scalar.activation(
                sig[:].rearrange("s (u p v) -> s u p v", u=2, v=2),
                acc1[:].rearrange("s (p u v) -> s u p v", u=2, v=2),
                SIGMOID,
            )
            h = ring.tile([P, H], BF16, name="h", align_bytes=64)
            nc.vector.tensor_tensor(
                h[:].rearrange("s (u p v) -> s u p v", u=2, v=2),
                acc3[:].rearrange("s (p u v) -> s u p v", u=2, v=2),
                sig[:].rearrange("s (u p v) -> s u p v", u=2, v=2),
                MULT,
            )
            hidden[j] = h

        def turn_and_quantise(pair):
            turned = take(scalar_banks)
            for side, j in enumerate(pair):
                value_pairs = hidden[j][:].bitcast(F32)
                for u in range(2):
                    at = (2 * side + u) * P
                    nc.tensor.transpose(turned[:, at : at + P], value_pairs[:, u * P : (u + 1) * P], ident[:])
            ht = ring.tile([P, 2 * BLOCK * 4], BF16, name="ht", align_bytes=64, bufs=TURNED_BUFS)
            nc.scalar.copy(
                ht[:].bitcast(F32).rearrange("p (side s u) -> p side s u", side=2, u=2),
                turned[:].rearrange("p (side u s) -> p side s u", side=2, u=2),
            )
            cols = slice(pair[0] * BLOCK, (pair[1] + 1) * BLOCK)
            nc.vector.quantize_mx(out=hw[:, cols].bitcast(FP8X4), scales=hs[:, cols], in_=ht[:])

        def second_product(acc, e, lo, hi):
            nc.tensor.matmul_mx(
                out=acc,
                lhsT=w2[:, e * 2 * N : (e + 1) * 2 * N].bitcast(FP4X4),
                lhsT_scale=s2[:, e * N : (e + 1) * N],
                rhs=hw[:, lo:hi].bitcast(FP8X4),
                rhs_scale=hs[:, lo:hi],
                start=True,
                stop=True,
            )

        def scatter_routed(pair):
            acc = take(held_banks)
            for side, e in enumerate(pair):
                second_product(acc[:, side * C : (side + 1) * C], e, e * C, (e + 1) * C)
            lo, hi = pair[0] * C, (pair[1] + 1) * C
            nc.scalar.copy(y[:, lo:hi], acc[:, : hi - lo])
            nc.vector.tensor_tensor(routed[:].indirect(list_slice(lo, hi)), y[:, lo:hi], gates[:, lo:hi], MULT)

        def add_shared_and_store(lo, hi):
            acc = take(held_banks)
            second_product(acc[:, : hi - lo], E, SLOTS + lo, SLOTS + hi)
            res = keep.tile([P, hi - lo], F32, name="res%d" % lo)
            nc.vector.tensor_tensor(res[:], acc[:, : hi - lo], routed[:, lo:hi], ADD)
            nc.sync.dma_start(out=out[:, lo:hi], in_=res[:])

        for pair in PAIRS[:AHEAD]:
            for j in pair:
                first_products(j)
        for step, pair in enumerate(PAIRS):
            if step + AHEAD < len(PAIRS):
                for j in PAIRS[step + AHEAD]:
                    first_products(j)
            turn_and_quantise(pair)
            if step >= LAG and PAIRS[step - LAG] in ROUTED_PAIRS:
                scatter_routed(PAIRS[step - LAG])
        for lo in range(0, T, BANK):
            add_shared_and_store(lo, min(lo + BANK, T))
